import numpy as np, ml_dtypes
CORES = [10,18,34,42,58,66,82,90,98,106]
N = 10
import mx_ref
NC, G = 256, 4
C = np.float32(0.037)
CNT = [[56,0,0,24,0,24,8,96,48,0],[0,72,0,64,40,0,32,32,0,16],[16,8,24,8,32,24,16,0,48,80],[64,56,32,0,0,16,64,0,24,0],[48,16,0,24,8,0,80,32,32,16],[40,16,80,56,0,40,0,0,0,24],[0,0,32,56,56,72,0,0,40,0],[8,48,0,16,32,0,24,32,48,48],[24,0,64,8,0,0,32,48,8,72],[0,40,24,0,88,80,0,16,8,0]]
OFF = [[sum(c[:e]) for e in range(N + 1)] for c in CNT]
BF = ml_dtypes.bfloat16
def cut(t, i, w=512):
    return t[:, w * i:w * i + w]
def tile(rs):
    return np.stack(rs, axis=2).reshape(128, -1).astype(BF)
def layer(w, X):
    out = []
    for i in range(G):
        for t in range(len(X)):
            p = mx_ref.matmul(mx_ref.quantize(cut(w, len(X) * i + t)), X[t])
            z = p if t == 0 else z + p
        out.append(z)
    return out
def act(Z):
    return [np.maximum(z, 0) * C for z in Z]
def setup_inputs(rng):
    def f(*shape):
        return mx_ref.flush((rng.standard_normal(shape, dtype=np.float32) * np.exp2(rng.integers(-2, 3, shape[:-1] + (1,)))).astype(BF))
    return {"x": f(N, 128, 4 * NC), "w1": f(N, 128, G * 512), "w2": f(N, 128, 512)}
def setup_inputs_blocks(rng):
    d = setup_inputs(rng)
    for k in ("x", "w1", "w2"): d[k] = mx_ref.spread(d[k], rng, 4)
    return d
def setup_inputs_wide(rng):
    d = setup_inputs(rng)
    for k in ("x", "w1", "w2"): d[k] = mx_ref.flush((d[k].astype(np.float32) * np.exp2(rng.integers(-8, 9, (N, 1, 1))).astype(np.float32)).astype(BF))
    return d
def setup_inputs_zeros(rng):
    d = setup_inputs(rng); v = d["x"].reshape(N, 128, -1, 4).copy()
    v[np.broadcast_to((rng.random((N, 1, v.shape[2], 1)) < 0.33), v.shape)] = 0
    d["x"] = v.reshape(d["x"].shape)
    return d
def reference(x, w1, w2):
    y = np.zeros((N, 128, NC), np.float32)
    for e in range(N):
        t = np.concatenate([x[j][:, 4 * OFF[j][e]:4 * OFF[j][e + 1]] for j in range(N)], axis=1)
        p = mx_ref.matmul(mx_ref.quantize(w2[e]), mx_ref.quantize(tile(act(layer(w1[e], [mx_ref.quantize(t)])))))
        c = 0
        for j in range(N):
            a, b = OFF[j][e], OFF[j][e + 1]
            y[j][:, a:b] = p[:, c:c + b - a]; c += b - a
    return {"y": y}

from concourse.bass import DstId, RemoteDMATransfer
from concourse.mybir import dt, AluOpType, ActivationFunctionType

NC = 256
COEF = 0.037
BANK = 512
NPH = 2
CFG = dict(
    helpers=0,
    share=0.5,
    hop=3.0,
    theta=(0.5,),
    other_die=True,
    fuse=True,
    halves=True,
)

SCRATCH = {
    "xb": ("sbuf", [128, 4 * NC], "bfloat16"),
    "w1b": ("sbuf", [128, 2048], "bfloat16"),
    "w2b": ("sbuf", [128, 512], "bfloat16"),
    "xq": ("sbuf", [128, 2 * NC], "float8_e4m3fn_x4"),
    "xs": ("sbuf", [128, 2 * NC], "uint8"),
    "w1q": ("sbuf", [128, 512], "float8_e4m3fn_x4"),
    "w1s": ("sbuf", [128, 512], "uint8"),
    "w2q": ("sbuf", [128, 128], "float8_e4m3fn_x4"),
    "w2s": ("sbuf", [128, 128], "uint8"),
    "ps": ("sbuf", [128, NC], "float32"),
    "yl": ("sbuf", [128, NC], "float32"),
    "z": ("psum", [128, 8 * BANK], "float32"),
}
SEMAPHORES = ["xl0", "xl1", "w1l", "w2l", "xqd0", "xqd1", "wq1", "wq2", "yown", "yarr", "sent", "stored", "fed"]
for _k in range(NPH):
    SCRATCH["hb%d" % _k] = ("sbuf", [128, 4 * NC], "bfloat16")
    SCRATCH["hq%d" % _k] = ("sbuf", [128, NC], "float8_e4m3fn_x4")
    SCRATCH["hs%d" % _k] = ("sbuf", [128, NC], "uint8")
    SEMAPHORES += ["arr%d" % _k, "act%d" % _k, "hqd%d" % _k, "pd%d" % _k, "psd%d" % _k]
    SEMAPHORES += ["z%d%d" % (_k, _b) for _b in range(4)]


def _fuse(writes, width):
    calls, left = [], list(writes)
    while left:
        same = [w for w in left if w["bytes"] == left[0]["bytes"] and w.get("late") == left[0].get("late")] if CFG["fuse"] else left[:1]
        take = 1
        while take * 2 <= min(len(same), width):
            take *= 2
        call = same[:take]
        for w in call:
            left.remove(w)
            w["eng"] = width // take
        calls.append(call)
    return calls


def _plan(CNT, width, fwidth):
    N, H = len(CNT), CFG["helpers"]
    OFF = [[sum(r[:e]) for e in range(N + 1)] for r in CNT]
    loads, tpos, order = [], [], []
    for j in range(N):
        cut = OFF[j][j + 1]
        loads.append([(0, 0, NC)] if cut == NC else [(0, cut, NC - cut), (NC - cut, 0, cut)])
        tpos.append([OFF[j][e] - cut if OFF[j][e] >= cut else OFF[j][e] + NC - cut for e in range(N)])
        ds = [(j + d) % N for d in range(1, N) if CNT[j][(j + d) % N] > 0]
        nmain = len(ds) if H == 0 else int(len(ds) * CFG["share"] + 0.5)
        rows = []
        for i, e in enumerate(ds):
            if i < nmain:
                rows.append(dict(e=e, ag=0, est=float(i)))
            else:
                r, per = i - nmain, -(-(len(ds) - nmain) // H)
                rows.append(dict(e=e, ag=1 + r // per, est=CFG["hop"] + r % per))
        order.append(rows)
    slot, bounds, members = [], [], []
    for e in range(N):
        inc = sorted((r["est"], (e - j) % N, j) for j in range(N) for r in order[j] if r["e"] == e)
        pos, sl, bd, mem, k = CNT[e][e], {}, [0], [[] for _ in range(NPH)], 0
        for i, (est, dist, j) in enumerate(inc):
            while k < NPH - 1 and i >= CFG["theta"][k] * len(inc):
                bd.append(pos)
                k += 1
            sl[j] = pos
            pos += CNT[j][e]
            mem[k].append(j)
        while len(bd) < NPH + 1:
            bd.append(pos)
        slot.append(sl); bounds.append(bd); members.append(mem)
    phase = [{j: k for k in range(NPH) for j in members[e][k]} for e in range(N)]
    disp, feed, ret = [], [], []
    for j in range(N):
        per_agent, fd = [], []
        for a in range(H + 1):
            mine = [r["e"] for r in order[j] if r["ag"] == a]
            calls = []
            for k in range(NPH):
                ws = []
                for e in mine:
                    if phase[e][j] == k:
                        n, dcol = CNT[j][e], NC - CNT[e][e] + slot[e][j]
                        late = tpos[j][e] + n > NC // 2
                        ws.append(dict(kind="c", to=e, src=tpos[j][e], dst=dcol, n=n, bytes=4 * n, ph=k, late=late))
                        ws.append(dict(kind="s", to=e, src=tpos[j][e], dst=dcol, n=n, bytes=n, ph=k, late=late))
                calls += _fuse(ws, width)
            per_agent.append(calls)
            if a > 0 and mine:
                lo = min(tpos[j][e] for e in mine)
                hi = max(tpos[j][e] + CNT[j][e] for e in mine)
                fd.append([dict(kind="fc", to=a, src=lo, dst=lo, n=hi - lo, bytes=4 * (hi - lo), eng=fwidth)])
                fd.append([dict(kind="fs", to=a, src=lo, dst=lo, n=hi - lo, bytes=hi - lo, eng=fwidth)])
        disp.append(per_agent); feed.append(fd)
    for e in range(N):
        ret.append([_fuse([dict(kind="y", to=j, src=slot[e][j], dst=OFF[j][e], n=CNT[j][e], bytes=4 * CNT[j][e], ph=k)
                           for j in members[e][k]], width) for k in range(NPH)])
    arr = [[0] * NPH for _ in range(N)]
    yarr, sent = [0] * N, [[0] * (H + 1) for _ in range(N)]
    for j in range(N):
        for a in range(H + 1):
            for call in disp[j][a]:
                for w in call:
                    sent[j][a] += w["eng"]
                    arr[w["to"]][w["ph"]] += w["eng"]
        for call in feed[j]:
            sent[j][0] += call[0]["eng"]
        for k in range(NPH):
            for call in ret[j][k]:
                for w in call:
                    sent[j][0] += w["eng"]
                    yarr[w["to"]] += w["eng"]
    return dict(OFF=OFF, loads=loads, bounds=bounds, disp=disp, feed=feed, ret=ret, arr=arr, yarr=yarr, sent=sent)


def _bits(m):
    return [b for b in range(16) if (m >> b) & 1]


def _helpers(c, T, topo):
    out = [h for h in range(max(T.cores) + 1) if h != c and topo.chip(h) == topo.chip(c) and T.rank_of(h) is None
           and all(topo.may_write(h, d) for d in T.cores)]
    far = [h for h in out if topo.die(h) != topo.die(c)]
    near = [h for h in out if topo.die(h) == topo.die(c)]
    return (far + near if CFG["other_die"] else near + far)[:CFG["helpers"]]


def rank_program(g, core, T, topo):
    CNT, S, cores = T.tables["CNT"], T.sem, T.cores
    me, agent = T.rank_of(core), 0
    if me is None:
        for j, c in enumerate(cores):
            hs = _helpers(c, T, topo)
            if core in hs:
                me, agent = j, 1 + hs.index(core)
        if me is None:
            return
    main = cores[me]
    helpers = _helpers(main, T, topo)
    off = None
    for c in cores:
        if c != main:
            off = topo.mask(core, c) if off is None else off & topo.mask(core, c)
    engines = _bits(off)
    fengines = []
    if helpers:
        on = _bits(topo.mask(main, helpers[0]))
        fengines = [b for b in on if b not in engines] or on
    P = _plan(CNT, len(engines), len(fengines))

    def emit(call):
        trs, nxt = [], 0
        for w in call:
            pool = fengines if w["kind"] in ("fc", "fs") else engines
            m = 0
            for b in pool[nxt:nxt + w["eng"]]:
                m |= 1 << b
            nxt += w["eng"]
            a, d, n = w["src"], w["dst"], w["n"]
            to = helpers[w["to"] - 1] if w["kind"] in ("fc", "fs") else cores[w["to"]]
            if w["kind"] in ("c", "fc"):
                src, dst = T.xq[:, a:a + n].bitcast(dt.uint8), T.xq[:, d:d + n].bitcast(dt.uint8)
            elif w["kind"] in ("s", "fs"):
                src, dst = T.xs[:, a:a + n], T.xs[:, d:d + n]
            else:
                src, dst = T.ps[:, a:a + n], T.yl[:, d:d + n]
            rs = S.fed if w["kind"] in ("fc", "fs") else S.yarr if w["kind"] == "y" else S["arr%d" % w["ph"]]
            rid, pid, _ = topo.addr(to)
            trs.append((src, dst, rs, rid, pid, m))
        if len(trs) == 1:
            src, dst, rs, rid, pid, m = trs[0]
            g.remote_dma(dst, src, rs, S.sent, pid, rid, m)
        else:
            g.remote_dma_fused([RemoteDMATransfer(dst_ids=[DstId(rid=rid, pnc=pid)], dma_engine_mask=m, remote_sem=rs, src=src, dst=dst)
                                for (src, dst, rs, rid, pid, m) in trs], local_sem=S.sent)

    if agent > 0:
        if P["disp"][me][agent]:
            g.wait_ge(S.fed, 2 * len(fengines))
            for call in P["disp"][me][agent]:
                emit(call)
            g.wait_ge(S.sent, P["sent"][me][agent])
        return

    own = CNT[me][me]
    base = NC - own
    v, sc, te, sy = g.vector, g.scalar, g.tensor, g.sync

    lq, nl, hw = [sy, sc], [0, 0], NC // 2
    for (tc, xc, n) in P["loads"][me]:
        cuts = [(tc, xc, n)] if not CFG["halves"] or tc >= hw or tc + n <= hw else [(tc, xc, hw - tc), (hw, xc + hw - tc, tc + n - hw)]
        for (a, b, m) in cuts:
            h = 1 if a >= hw else 0
            lq[h].dma_start(T.xb[:, 4 * a:4 * (a + m)], T.x[:, 4 * b:4 * (b + m)]).then_inc(S["xl%d" % h], 16)
            nl[h] += 16
    sy.dma_start(T.w1b[:], T.w1[:]).then_inc(S.w1l, 16)
    sc.dma_start(T.w2b[:], T.w2[:]).then_inc(S.w2l, 16)
    if CFG["halves"]:
        for h in range(2):
            v.wait_ge(S["xl%d" % h], nl[h])
            v.quantize_mx(T.xq[:, h * hw:h * hw + hw], T.xs[:, h * hw:h * hw + hw], T.xb[:, 4 * h * hw:4 * (h * hw + hw)]).then_inc(S["xqd%d" % h], 1)
    else:
        for h in range(2):
            if nl[h]:
                v.wait_ge(S["xl%d" % h], nl[h])
        v.quantize_mx(T.xq[:, 0:NC], T.xs[:, 0:NC], T.xb[:]).then_inc(S.xqd1, 1)
    v.wait_ge(S.w1l, 16)
    v.quantize_mx(T.w1q[:], T.w1s[:], T.w1b[:]).then_inc(S.wq1, 1)
    v.wait_ge(S.w2l, 16)
    v.quantize_mx(T.w2q[:], T.w2s[:], T.w2b[:]).then_inc(S.wq2, 1)

    seen = not CFG["halves"]
    g.wait_ge(S.xqd1 if seen else S.xqd0, 1)
    for call in P["feed"][me] + P["disp"][me][0]:
        if not seen and call[0].get("late", True):
            g.wait_ge(S.xqd1, 1)
            seen = True
        emit(call)

    if CFG["halves"]:
        te.wait_ge(S.xqd0, 1)
    te.wait_ge(S.xqd1, 1)
    te.wait_ge(S.wq1, 1)
    te.wait_ge(S.wq2, 1)
    bd, freed = P["bounds"][me], {}
    for k in range(NPH):
        lo, hi = min(bd[k], bd[k + 1] - 128), bd[k + 1]
        if hi == bd[k]:
            continue
        n = hi - lo
        hb, hq, hs = T["hb%d" % k], T["hq%d" % k], T["hs%d" % k]
        b0 = 4 * (k % 2)
        if P["arr"][me][k]:
            te.wait_ge(S["arr%d" % k], P["arr"][me][k])
        for wsem in freed.get(k - 2, []):
            te.wait_ge(S[wsem], 1)
        for b in range(4):
            zc = (b0 + b) * BANK
            te.matmul_mx(T.z[:, zc:zc + n], T.w1q[:, 128 * b:128 * b + 128], T.w1s[:, 128 * b:128 * b + 128],
                         T.xq[:, base + lo:base + hi], T.xs[:, base + lo:base + hi], True, True).then_inc(S["z%d%d" % (k, b)], 1)
            if b % 2 == 0:
                v.wait_ge(S["z%d%d" % (k, b)], 1)
                v.tensor_scalar(hb[:, b:4 * n:4], T.z[:, zc:zc + n], 0.0, COEF, AluOpType.max, AluOpType.mult).then_inc(S["act%d" % k], 1)
            else:
                sc.wait_ge(S["z%d%d" % (k, b)], 1)
                sc.activation(hb[:, b:4 * n:4], T.z[:, zc:zc + n], ActivationFunctionType.Relu, scale=COEF).then_inc(S["act%d" % k], 1)
        v.wait_ge(S["act%d" % k], 4)
        v.quantize_mx(hq[:, 0:n], hs[:, 0:n], hb[:, 0:4 * n]).then_inc(S["hqd%d" % k], 1)
        te.wait_ge(S["hqd%d" % k], 1)
        pc = b0 * BANK
        te.matmul_mx(T.z[:, pc:pc + n], T.w2q[:], T.w2s[:], hq[:, 0:n], hs[:, 0:n], True, True).then_inc(S["pd%d" % k], 1)
        v.wait_ge(S["pd%d" % k], 1)
        first = max(bd[k], own)
        if hi > first:
            v.tensor_copy(T.ps[:, first:hi], T.z[:, pc + first - lo:pc + hi - lo]).then_inc(S["psd%d" % k], 1)
            g.wait_ge(S["psd%d" % k], 1)
            freed.setdefault(k, []).append("psd%d" % k)
            for call in P["ret"][me][k]:
                emit(call)
        if bd[k] < own:
            a = P["OFF"][me][me]
            v.tensor_copy(T.yl[:, a:a + own], T.z[:, pc - lo:pc - lo + own]).then_inc(S.yown, 1)
            freed.setdefault(k, []).append("yown")
    g.wait_ge(S.sent, P["sent"][me][0])

    if own:
        sy.wait_ge(S.yown, 1)
    sy.wait_ge(S.yarr, P["yarr"][me])
    sy.dma_start(T.y[:], T.yl[:]).then_inc(S.stored, 16)
    sy.wait_ge(S.stored, 16)
